import numpy as np
import ml_dtypes


def mxq(x, axis, fmt="e4m3"):
    dtype, down = {"e4m3": (ml_dtypes.float8_e4m3fn, 7), "e5m2": (ml_dtypes.float8_e5m2, 14)}[fmt]
    v = np.moveaxis(np.asarray(x, np.float32).astype(ml_dtypes.bfloat16).astype(np.float64), axis, -1)
    blocks = v.reshape(v.shape[:-1] + (-1, 32))
    amax = np.abs(blocks).max(-1, keepdims=True)
    byte = np.maximum(np.where(amax > 0, np.frexp(amax)[1] - 1 + 127, 0) - down, 1)
    scale = np.exp2(byte - 127.0)
    codes = (blocks / scale).astype(np.float32).astype(dtype).astype(np.float64)
    return np.moveaxis((codes * scale).reshape(v.shape), -1, axis)


WIDE = False


def mx_kscale(k):
    if not WIDE:
        return np.ones(k)
    levels = np.array([30, -30])
    if k % 512:
        return np.exp2(np.random.permutation(np.resize(levels, k // 32))).repeat(32)
    a = np.empty((k // 512, 16))
    for p in range(k // 512):
        a[p, :8] = np.random.permutation(np.resize(levels, 8))
        for g in range(8):
            far = levels[np.abs(levels - a[p, g]) >= 10]
            a[p, g + 8] = far[np.random.randint(len(far))]
    return np.exp2(a.ravel()).repeat(32)


BF16 = ml_dtypes.bfloat16


def bf(x):
    return np.asarray(x, np.float32).astype(BF16)


def f64(x):
    return np.asarray(x).astype(np.float64)


E2M1 = np.array([0.0, 0.5, 1.0, 1.5, 2.0, 3.0, 4.0, 6.0, -0.0, -0.5, -1.0, -1.5, -2.0, -3.0, -4.0, -6.0])


def pack_weight(w, fmt):
    k, n = w.shape
    w = f64(bf(w)).reshape(k // 32, 32, n)
    amax = np.abs(w).max(1)
    if fmt in ("e4m3", "e5m2"):
        byte = np.frexp(amax)[1] - 1 + 127 - (7 if fmt == "e4m3" else 14)
    else:
        mant, ex = np.frexp(amax / 6.0)
        byte = np.where(mant > 0.5, ex, ex - 1) + 127
    byte = np.clip(np.where(amax > 0, byte, 1), 1, 254)
    scaled = (w * np.exp2(127.0 - byte)[:, None, :]).reshape(k, n).astype(np.float32)
    by_word = np.ascontiguousarray(scaled.reshape(k // 512, 128, 4, n).transpose(0, 1, 3, 2))
    if fmt in ("e4m3", "e5m2"):
        words = by_word.astype(ml_dtypes.float8_e4m3fn if fmt == "e4m3" else ml_dtypes.float8_e5m2).view(np.uint8)
    else:
        c = by_word.astype(ml_dtypes.float4_e2m1fn).view(np.uint8) & 0xF
        words = c[..., 0::2] | (c[..., 1::2] << 4)
    return np.ascontiguousarray(words), np.ascontiguousarray(byte.astype(np.uint8).reshape(k // 512, 16, n))


def unpack_weight(words, scales, fmt):
    g, p, n, _ = words.shape
    if fmt in ("e4m3", "e5m2"):
        vals = np.ascontiguousarray(words).view(ml_dtypes.float8_e4m3fn if fmt == "e4m3" else ml_dtypes.float8_e5m2).astype(np.float64)
    else:
        nib = np.empty((g, p, n, 4), np.uint8)
        nib[..., 0::2] = words & 0xF
        nib[..., 1::2] = words >> 4
        vals = E2M1[nib]
    vals = vals * np.repeat(np.exp2(scales.astype(np.float64) - 127.0), 8, axis=1)[..., None]
    return vals.transpose(0, 1, 3, 2).reshape(g * 512, n)

def planes(Y):
    n, m = Y.shape
    b = f64(bf(Y)).reshape(n // 32, 32, m)
    amax = np.abs(b).max(1)
    byte = np.clip(np.where(amax > 0, np.frexp(amax)[1] - 1 + 127 - 7, 1), 1, 254)
    codes = (b * np.exp2(127.0 - byte)[:, None, :]).reshape(n, m).astype(np.float32).astype(ml_dtypes.float8_e4m3fn).view(np.uint8)
    words = codes.reshape(n // 512, 128, 4, m).transpose(0, 1, 3, 2)
    return np.ascontiguousarray(words), np.ascontiguousarray(byte.astype(np.uint8).reshape(n // 512, 16, m))


NI, NX, NB, NY = 1024, 1024, 4, 512


def setup_inputs():
    s = mx_kscale(NX)
    spread = np.exp(0.8 * np.random.randn(NI))
    a = spread[:, None] * np.random.randn(NI, NX) / np.sqrt(NX)
    g = np.random.standard_t(3.0, (NX, NB * NY))
    g_words, g_scales = pack_weight(g / s[:, None], "e5m2")
    u = 0.8 * spread[:, None, None] * np.random.randn(NI, NB, NY)
    return {
        "g_words": g_words,
        "g_scales": g_scales,
        "a": bf(a * s[None, :]),
        "lam": bf(0.6 * np.exp(0.5 * np.random.randn(NI))),
        "kappa": bf(0.6 * np.exp(0.5 * np.random.randn(NB))),
        "mu": bf(0.6 * np.exp(0.5 * np.random.randn(NY))),
        "u": bf(u),
    }

def reference(g_words, g_scales, a, lam, kappa, mu, u):
    G = unpack_weight(g_words, g_scales, "e5m2")
    h = (mxq(f64(a), 1, "e4m3") @ G).reshape(NI, NB, NY)
    d = f64(lam)[:, None, None] + f64(kappa)[None, :, None] + f64(mu)[None, None, :]
    y = f64(u) + h / d
    Y = y.reshape(NI, NB * NY)
    words, scales = planes(Y)
    return y, words, scales

@@ -1,0 +1,265 @@
+from contextlib import ExitStack
+
+import concourse.mybir as mybir
+from concourse.masks import make_identity
+
+NI, NX, NB, NY = 1024, 1024, 4, 512
+FLOPS = 2 * NI * NX * NB * NY
+
+F32 = mybir.dt.float32
+BF16 = mybir.dt.bfloat16
+I32 = mybir.dt.int32
+U32 = mybir.dt.uint32
+U8 = mybir.dt.uint8
+E4M3 = mybir.dt.float8_e4m3fn_x4
+E5M2 = mybir.dt.float8_e5m2_x4
+ALU = mybir.AluOpType
+ACT = mybir.ActivationFunctionType
+
+P = 128
+PACK = 4
+GROUP = P * PACK
+PASSES = NX // GROUP
+GROUPS = NI // GROUP
+TILES = GROUPS * NB
+BANKS = 8
+HALF = NY // 2
+
+
+def tile_second_side_rate_division_k2_kernel(tc, g_words, g_scales, a, lam, kappa, mu, u, out_0, out_1, out_2):
+    nc = tc.nc
+    with ExitStack() as ctx:
+        keep = ctx.enter_context(tc.tile_pool(name="keep", bufs=1))
+        ring = ctx.enter_context(tc.tile_pool(name="ring", bufs=4))
+        psum = ctx.enter_context(tc.psum_pool(name="psum", bufs=1))
+        ctx.enter_context(tc.manual_schedule())
+
+        banks_taken = []
+
+        def next_bank():
+            n = len(banks_taken)
+            banks_taken.append(n)
+            return psum.tile([P, NY], F32, name="bank%d" % n, tag="bank%d" % (n % BANKS))
+
+        def kept(name, shape, dtype):
+            return keep.tile(shape, dtype, name=name, tag=name, align_bytes=64)
+
+        slots = [(g, t) for g in range(GROUPS) for t in range(PACK)]
+        a_rows = a.rearrange("(g m t) x -> g m t x", g=GROUPS, t=PACK)
+        u_rows = u.rearrange("(g p t) b j -> g p t (b j)", g=GROUPS, t=PACK)
+        y_rows = out_0.rearrange("(g p t) b j -> g p t b j", g=GROUPS, t=PACK)
+        g_cols = g_words.rearrange("q p n t -> p q (n t)")
+        g_scale_rows = g_scales.rearrange("q r n -> r q n")
+        y_words_out = out_1.rearrange("g p n t -> g p (n t)")
+
+        ident = kept("ident", [P, P], F32)
+        mu_sb = kept("mu_sb", [P, PACK], BF16)
+        lam_sb = kept("lam_sb", [P, GROUPS, 16], BF16)
+        kappa_sb = kept("kappa_sb", [P, NB], BF16)
+        row_rate = kept("row_rate", [P, GROUPS, NB, PACK], F32)
+        ln_row = kept("ln_row", [P, GROUPS, NB, PACK], F32)
+        inv_row = kept("inv_row", [P, GROUPS, NB, PACK], F32)
+        ln_mu_col = kept("ln_mu_col", [P, PACK], F32)
+        ln_mu = kept("ln_mu", [P, NY], F32)
+        g_plane = kept("g_plane", [P, PASSES, NB * NY], U8)
+        g_codes = [kept("g_codes%d" % b, [P, PASSES, NY], U32) for b in range(NB)]
+        a_raw0 = [kept("a_raw0_%d" % h, [P, 2, NX], BF16) for h in range(2)]
+        a_raw1 = kept("a_raw1", [P, PACK, NX], BF16)
+        a_codes = {s: kept("a_codes%d%d" % s, [P, PASSES * P], U32) for s in slots}
+        a_plane = {s: kept("a_plane%d%d" % s, [P, PASSES * P], U8) for s in slots}
+        a_grouped = {s: kept("a_grouped%d%d" % s, [P, PASSES * P * PACK], BF16) for s in slots}
+        u_sb = [kept("u_sb%d" % c, [P, PACK, 2 * NY], BF16) for c in range(TILES // 2)]
+        y_sb = [kept("y_sb%d" % k, [P, PACK, NY], F32) for k in range(TILES)]
+        y_codes = [kept("y_codes%d" % k, [P, NY], U32) for k in range(TILES)]
+        y_plane = [kept("y_plane%d" % g, [P, NB * NY], U8) for g in range(GROUPS)]
+
+        a_bank, h_bank, share, y_grouped = {}, {}, {}, {}
+
+        def load_g(b):
+            nc.sync.dma_start(out=g_codes[b][:].bitcast(I32),
+                              in_=g_cols[:, :, b * NY * PACK:(b + 1) * NY * PACK].bitcast(I32))
+
+        def load_u(c):
+            g, h = divmod(c, 2)
+            nc.sync.dma_start(out=u_sb[c][:], in_=u_rows[g][:, :, h * 2 * NY:(h + 1) * 2 * NY])
+
+        def turn_a(g, t):
+            raw = a_raw0[t // 2][:, t % 2, :] if g == 0 else a_raw1[:, t, :]
+            words = raw.bitcast(F32)
+            bank = next_bank()
+            a_bank[g, t] = bank
+            for q in range(PASSES):
+                for e in range(2):
+                    n = 2 * q + e
+                    nc.tensor.transpose(bank[:, n * P:(n + 1) * P],
+                                        words[:, 2 * P * q + e:2 * P * (q + 1):2], ident[:])
+
+        def group_a(g, t, copy):
+            copy(out=a_grouped[g, t][:].bitcast(F32).rearrange("p (q m e) -> p q m e", q=PASSES, e=2),
+                 in_=a_bank[g, t][:].rearrange("p (q e m) -> p q m e", q=PASSES, e=2))
+
+        def quantize_a(g, t):
+            nc.vector.quantize_mx(out=a_codes[g, t][:].bitcast(E4M3), scales=a_plane[g, t][:], in_=a_grouped[g, t][:])
+
+        def product(k, t):
+            g, b = divmod(k, NB)
+            bank = next_bank()
+            h_bank[k, t] = bank
+            for q in range(PASSES):
+                nc.tensor.matmul_mx(
+                    out=bank[:],
+                    lhsT=a_codes[g, t][:, q * P:(q + 1) * P].bitcast(E4M3),
+                    lhsT_scale=a_plane[g, t][:, q * P:(q + 1) * P],
+                    rhs=g_codes[b][:, q, :].bitcast(E5M2),
+                    rhs_scale=g_plane[:, q, b * NY:(b + 1) * NY],
+                    start=(q == 0), stop=(q == PASSES - 1))
+
+        def shares(k):
+            g, b = divmod(k, NB)
+            share[k] = ring.tile([P, PACK, NY], F32, name="share%d" % k, tag="share", align_bytes=64)
+            for t in range(PACK):
+                nc.scalar.activation(out=share[k][:, t, :], in_=ln_mu[:], func=ACT.Sigmoid,
+                                     scale=-1.0, bias=ln_row[:, g, b, t:t + 1])
+
+        def divide(k, t):
+            g, b = divmod(k, NB)
+            nc.vector.scalar_tensor_tensor(out=y_sb[k][:, t, :], in0=h_bank[k, t][:], scalar=inv_row[:, g, b, t:t + 1],
+                                           in1=share[k][:, t, :], op0=ALU.mult, op1=ALU.mult)
+
+        def add_u(k, t0, t1, j0, j1):
+            off = (k % 2) * NY
+            nc.vector.tensor_tensor(out=y_sb[k][:, t0:t1, j0:j1], in0=y_sb[k][:, t0:t1, j0:j1],
+                                    in1=u_sb[k // 2][:, t0:t1, off + j0:off + j1], op=ALU.add)
+
+        def group_y(k, j0, j1, copy):
+            tile_y = ring.tile([P, (j1 - j0) * PACK], BF16, name="y_grouped%d_%d" % (k, j0), tag="y_grouped", align_bytes=64)
+            y_grouped[k, j0] = tile_y
+            copy(out=tile_y[:].rearrange("p (c i t) -> p c t i", i=4, t=PACK),
+                 in_=y_sb[k][:, :, j0:j1].rearrange("p t (c i) -> p c t i", i=4))
+
+        def quantize_y(k, j0, j1):
+            g, b = divmod(k, NB)
+            nc.vector.quantize_mx(out=y_codes[k][:, j0:j1].bitcast(E4M3),
+                                  scales=y_plane[g][:, b * NY + j0:b * NY + j1], in_=y_grouped[k, j0][:])
+
+        def store_y(k, j0, j1):
+            g, b = divmod(k, NB)
+            nc.sync.dma_start(out=y_rows[g][:, :, b, j0:j1], in_=y_sb[k][:, :, j0:j1])
+
+        def store_codes(k, j0, j1):
+            g, b = divmod(k, NB)
+            c0, c1 = (b * NY + j0) * PACK, (b * NY + j1) * PACK
+            nc.sync.dma_start(out=y_words_out[g][:, c0:c1].bitcast(I32), in_=y_codes[k][:, j0:j1].bitcast(I32))
+
+        def store_scales(g, c0, c1, queues):
+            for quad in range(4):
+                queues[quad].dma_start(out=out_2[g][4 * quad:4 * quad + 4, c0:c1].bitcast(I32),
+                                       in_=y_plane[g][32 * quad:32 * quad + 4, c0:c1].bitcast(I32))
+
+        nc.vector.memset(g_plane[:].rearrange("p q n -> p (q n)").bitcast(I32), 0)
+        make_identity(nc, ident[:])
+        nc.sync.dma_start(out=mu_sb[:], in_=mu.rearrange("(p t) -> p t", t=PACK))
+        nc.sync.dma_start(out=lam_sb[:, :, 0:PACK], in_=lam.rearrange("(g p t) -> p g t", g=GROUPS, t=PACK))
+        nc.sync.dma_start(out=kappa_sb[:], in_=kappa.partition_broadcast(P))
+        nc.sync.dma_start(out=a_raw0[0][:], in_=a_rows[0][:, 0:2, :])
+        for quad in range(4):
+            nc.sync.dma_start(out=g_plane[32 * quad:32 * quad + 4, :, :].bitcast(I32),
+                              in_=g_scale_rows[4 * quad:4 * quad + 4].bitcast(I32))
+        load_g(0)
+        nc.sync.dma_start(out=a_raw0[1][:], in_=a_rows[0][:, 2:4, :])
+        load_u(0)
+        load_g(1)
+        load_g(2)
+        load_u(1)
+        load_g(3)
+        nc.sync.dma_start(out=a_raw1[:], in_=a_rows[1])
+        load_u(2)
+        load_u(3)
+
+        nc.scalar.activation(out=ln_mu_col[:], in_=mu_sb[:], func=ACT.Ln)
+        for b in range(NB):
+            nc.vector.tensor_scalar(out=row_rate[:, :, b, :], in0=lam_sb[:, :, 0:PACK], scalar1=kappa_sb[:, b:b + 1],
+                                    scalar2=None, op0=ALU.add)
+        nc.scalar.activation(out=ln_row[:].rearrange("p g b t -> p (g b t)"),
+                             in_=row_rate[:].rearrange("p g b t -> p (g b t)"), func=ACT.Ln)
+        nc.vector.reciprocal(out=inv_row[:].rearrange("p g b t -> p (g b t)"),
+                             in_=row_rate[:].rearrange("p g b t -> p (g b t)"))
+        mu_bank = next_bank()
+        for t in range(PACK):
+            nc.tensor.transpose(mu_bank[:, t * P:(t + 1) * P], ln_mu_col[:, t:t + 1].to_broadcast([P, P]), ident[:])
+        nc.vector.tensor_copy(out=ln_mu[:].rearrange("p (n t) -> p n t", t=PACK),
+                              in_=mu_bank[:].rearrange("p (t n) -> p n t", t=PACK))
+        shares(0)
+        shares(1)
+        shares(2)
+
+        turn_a(0, 0)
+        turn_a(0, 1)
+        group_a(0, 0, nc.vector.tensor_copy)
+        group_a(0, 1, nc.vector.tensor_copy)
+        quantize_a(0, 0)
+        quantize_a(0, 1)
+        product(0, 0)
+        turn_a(0, 2)
+        product(0, 1)
+        turn_a(0, 3)
+        divide(0, 0)
+        group_a(0, 2, nc.vector.tensor_copy)
+        divide(0, 1)
+        group_a(0, 3, nc.vector.tensor_copy)
+        quantize_a(0, 2)
+        quantize_a(0, 3)
+        product(0, 2)
+        product(0, 3)
+        add_u(0, 0, 2, 0, NY)
+        divide(0, 2)
+        divide(0, 3)
+        for t in range(PACK):
+            product(1, t)
+        divide(1, 0)
+        add_u(0, 2, 4, 0, NY)
+        store_y(0, 0, NY)
+        group_y(0, 0, NY, nc.scalar.copy)
+        shares(3)
+
+        last = TILES - 1
+        for k in range(1, TILES):
+            for t in range(PACK):
+                if (k, t) != (1, 0):
+                    divide(k, t)
+                if k < last:
+                    product(k + 1, t)
+            if k == 1:
+                for t in range(PACK):
+                    turn_a(1, t)
+            add_u(k, 0, 2, 0, NY)
+            quantize_y(k - 1, 0, NY)
+            store_codes(k - 1, 0, NY)
+            if k - 1 == NB - 1:
+                store_scales(0, 0, NB * NY, [nc.sync] * 4)
+            if k - 1 == NB + 1:
+                store_scales(1, 0, 2 * NY, [nc.sync] * 4)
+            if k < last:
+                add_u(k, 2, 4, 0, NY)
+                store_y(k, 0, NY)
+                group_y(k, 0, NY, nc.scalar.copy)
+                if k == 1:
+                    for t in range(PACK):
+                        group_a(1, t, nc.scalar.copy)
+                elif k + 2 < TILES:
+                    shares(k + 2)
+            if k == 2:
+                for t in range(PACK):
+                    quantize_a(1, t)
+
+        add_u(last, 2, 4, 0, HALF)
+        store_y(last, 0, HALF)
+        group_y(last, 0, HALF, nc.scalar.copy)
+        add_u(last, 2, 4, HALF, NY)
+        store_y(last, HALF, NY)
+        group_y(last, HALF, NY, nc.vector.tensor_copy)
+        quantize_y(last, 0, HALF)
+        store_codes(last, 0, HALF)
+        quantize_y(last, HALF, NY)
+        store_codes(last, HALF, NY)
+        store_scales(1, 2 * NY, NB * NY, [nc.sync, nc.sync, nc.scalar, nc.scalar])

@@ -44,7 +44,7 @@ def tile_second_side_rate_division_k2_kernel(tc, g_words, g_scales, a, lam, kapp
         def kept(name, shape, dtype):
             return keep.tile(shape, dtype, name=name, tag=name, align_bytes=64)
 
-        slots = [(g, t) for g in range(GROUPS) for t in range(PACK)]
+        slots = [(g, h) for g in range(GROUPS) for h in range(2)]
         a_rows = a.rearrange("(g m t) x -> g m t x", g=GROUPS, t=PACK)
         u_rows = u.rearrange("(g p t) b j -> g p t (b j)", g=GROUPS, t=PACK)
         y_rows = out_0.rearrange("(g p t) b j -> g p t b j", g=GROUPS, t=PACK)
@@ -59,17 +59,16 @@ def tile_second_side_rate_division_k2_kernel(tc, g_words, g_scales, a, lam, kapp
         row_rate = kept("row_rate", [P, GROUPS, NB, PACK], F32)
         ln_row = kept("ln_row", [P, GROUPS, NB, PACK], F32)
         inv_row = kept("inv_row", [P, GROUPS, NB, PACK], F32)
-        ln_mu_col = kept("ln_mu_col", [P, PACK], F32)
         ln_mu = kept("ln_mu", [P, NY], F32)
         g_plane = kept("g_plane", [P, PASSES, NB * NY], U8)
         g_codes = [kept("g_codes%d" % b, [P, PASSES, NY], U32) for b in range(NB)]
         a_raw0 = [kept("a_raw0_%d" % h, [P, 2, NX], BF16) for h in range(2)]
         a_raw1 = kept("a_raw1", [P, PACK, NX], BF16)
-        a_codes = {s: kept("a_codes%d%d" % s, [P, PASSES * P], U32) for s in slots}
-        a_plane = {s: kept("a_plane%d%d" % s, [P, PASSES * P], U8) for s in slots}
-        a_grouped = {s: kept("a_grouped%d%d" % s, [P, PASSES * P * PACK], BF16) for s in slots}
+        a_codes = {s: kept("a_codes%d%d" % s, [P, 2, PASSES * P], U32) for s in slots}
+        a_plane = {s: kept("a_plane%d%d" % s, [P, 2, PASSES * P], U8) for s in slots}
+        a_grouped = {s: kept("a_grouped%d%d" % s, [P, 2, PASSES * P * PACK], BF16) for s in slots}
         u_sb = [kept("u_sb%d" % c, [P, PACK, 2 * NY], BF16) for c in range(TILES // 2)]
-        y_sb = [kept("y_sb%d" % k, [P, PACK, NY], F32) for k in range(TILES)]
+        y_sb = [kept("y_sb%d" % c, [P, PACK, 2 * NY], F32) for c in range(TILES // 2)]
         y_codes = [kept("y_codes%d" % k, [P, NY], U32) for k in range(TILES)]
         y_plane = [kept("y_plane%d" % g, [P, NB * NY], U8) for g in range(GROUPS)]
 
@@ -79,9 +78,9 @@ def tile_second_side_rate_division_k2_kernel(tc, g_words, g_scales, a, lam, kapp
             nc.sync.dma_start(out=g_codes[b][:].bitcast(I32),
                               in_=g_cols[:, :, b * NY * PACK:(b + 1) * NY * PACK].bitcast(I32))
 
-        def load_u(c):
+        def load_u(c, t0, t1):
             g, h = divmod(c, 2)
-            nc.sync.dma_start(out=u_sb[c][:], in_=u_rows[g][:, :, h * 2 * NY:(h + 1) * 2 * NY])
+            nc.sync.dma_start(out=u_sb[c][:, t0:t1, :], in_=u_rows[g][:, t0:t1, h * 2 * NY:(h + 1) * 2 * NY])
 
         def turn_a(g, t):
             raw = a_raw0[t // 2][:, t % 2, :] if g == 0 else a_raw1[:, t, :]
@@ -95,11 +94,13 @@ def tile_second_side_rate_division_k2_kernel(tc, g_words, g_scales, a, lam, kapp
                                         words[:, 2 * P * q + e:2 * P * (q + 1):2], ident[:])
 
         def group_a(g, t, copy):
-            copy(out=a_grouped[g, t][:].bitcast(F32).rearrange("p (q m e) -> p q m e", q=PASSES, e=2),
+            copy(out=a_grouped[g, t // 2][:, t % 2, :].bitcast(F32).rearrange("p (q m e) -> p q m e", q=PASSES, e=2),
                  in_=a_bank[g, t][:].rearrange("p (q e m) -> p q m e", q=PASSES, e=2))
 
-        def quantize_a(g, t):
-            nc.vector.quantize_mx(out=a_codes[g, t][:].bitcast(E4M3), scales=a_plane[g, t][:], in_=a_grouped[g, t][:])
+        def quantize_a(g, h, s0, s1):
+            nc.vector.quantize_mx(out=a_codes[g, h][:, s0:s1, :].rearrange("p s n -> p (s n)").bitcast(E4M3),
+                                  scales=a_plane[g, h][:, s0:s1, :].rearrange("p s n -> p (s n)"),
+                                  in_=a_grouped[g, h][:, s0:s1, :].rearrange("p s n -> p (s n)"))
 
         def product(k, t):
             g, b = divmod(k, NB)
@@ -108,43 +109,47 @@ def tile_second_side_rate_division_k2_kernel(tc, g_words, g_scales, a, lam, kapp
             for q in range(PASSES):
                 nc.tensor.matmul_mx(
                     out=bank[:],
-                    lhsT=a_codes[g, t][:, q * P:(q + 1) * P].bitcast(E4M3),
-                    lhsT_scale=a_plane[g, t][:, q * P:(q + 1) * P],
+                    lhsT=a_codes[g, t // 2][:, t % 2, q * P:(q + 1) * P].bitcast(E4M3),
+                    lhsT_scale=a_plane[g, t // 2][:, t % 2, q * P:(q + 1) * P],
                     rhs=g_codes[b][:, q, :].bitcast(E5M2),
                     rhs_scale=g_plane[:, q, b * NY:(b + 1) * NY],
                     start=(q == 0), stop=(q == PASSES - 1))
 
-        def shares(k):
+        def shares(k, ts):
             g, b = divmod(k, NB)
-            share[k] = ring.tile([P, PACK, NY], F32, name="share%d" % k, tag="share", align_bytes=64)
-            for t in range(PACK):
+            if k not in share:
+                share[k] = ring.tile([P, PACK, NY], F32, name="share%d" % k, tag="share", align_bytes=64)
+            for t in ts:
                 nc.scalar.activation(out=share[k][:, t, :], in_=ln_mu[:], func=ACT.Sigmoid,
                                      scale=-1.0, bias=ln_row[:, g, b, t:t + 1])
 
+        def y_tile(k):
+            return y_sb[k // 2][:, :, (k % 2) * NY:(k % 2 + 1) * NY]
+
         def divide(k, t):
             g, b = divmod(k, NB)
-            nc.vector.scalar_tensor_tensor(out=y_sb[k][:, t, :], in0=h_bank[k, t][:], scalar=inv_row[:, g, b, t:t + 1],
+            nc.vector.scalar_tensor_tensor(out=y_tile(k)[:, t, :], in0=h_bank[k, t][:], scalar=inv_row[:, g, b, t:t + 1],
                                            in1=share[k][:, t, :], op0=ALU.mult, op1=ALU.mult)
 
-        def add_u(k, t0, t1, j0, j1):
+        def add_u(engine, k, t0, t1, j0, j1):
             off = (k % 2) * NY
-            nc.vector.tensor_tensor(out=y_sb[k][:, t0:t1, j0:j1], in0=y_sb[k][:, t0:t1, j0:j1],
-                                    in1=u_sb[k // 2][:, t0:t1, off + j0:off + j1], op=ALU.add)
+            engine.tensor_tensor(out=y_tile(k)[:, t0:t1, j0:j1], in0=y_tile(k)[:, t0:t1, j0:j1],
+                                 in1=u_sb[k // 2][:, t0:t1, off + j0:off + j1], op=ALU.add)
 
         def group_y(k, j0, j1, copy):
             tile_y = ring.tile([P, (j1 - j0) * PACK], BF16, name="y_grouped%d_%d" % (k, j0), tag="y_grouped", align_bytes=64)
             y_grouped[k, j0] = tile_y
             copy(out=tile_y[:].rearrange("p (c i t) -> p c t i", i=4, t=PACK),
-                 in_=y_sb[k][:, :, j0:j1].rearrange("p t (c i) -> p c t i", i=4))
+                 in_=y_tile(k)[:, :, j0:j1].rearrange("p t (c i) -> p c t i", i=4))
 
         def quantize_y(k, j0, j1):
             g, b = divmod(k, NB)
             nc.vector.quantize_mx(out=y_codes[k][:, j0:j1].bitcast(E4M3),
                                   scales=y_plane[g][:, b * NY + j0:b * NY + j1], in_=y_grouped[k, j0][:])
 
-        def store_y(k, j0, j1):
+        def store_y(k, t0, t1, j0, j1):
             g, b = divmod(k, NB)
-            nc.sync.dma_start(out=y_rows[g][:, :, b, j0:j1], in_=y_sb[k][:, :, j0:j1])
+            nc.sync.dma_start(out=y_rows[g][:, t0:t1, b, j0:j1], in_=y_tile(k)[:, t0:t1, j0:j1])
 
         def store_codes(k, j0, j1):
             g, b = divmod(k, NB)
@@ -161,105 +166,129 @@ def tile_second_side_rate_division_k2_kernel(tc, g_words, g_scales, a, lam, kapp
         nc.sync.dma_start(out=mu_sb[:], in_=mu.rearrange("(p t) -> p t", t=PACK))
         nc.sync.dma_start(out=lam_sb[:, :, 0:PACK], in_=lam.rearrange("(g p t) -> p g t", g=GROUPS, t=PACK))
         nc.sync.dma_start(out=kappa_sb[:], in_=kappa.partition_broadcast(P))
-        nc.sync.dma_start(out=a_raw0[0][:], in_=a_rows[0][:, 0:2, :])
+        nc.sync.dma_start(out=a_raw0[0][:, 0, :], in_=a_rows[0][:, 0, :])
+        nc.sync.dma_start(out=a_raw0[0][:, 1, :], in_=a_rows[0][:, 1, :])
+        nc.sync.dma_start(out=a_raw0[1][:], in_=a_rows[0][:, 2:4, :])
         for quad in range(4):
             nc.sync.dma_start(out=g_plane[32 * quad:32 * quad + 4, :, :].bitcast(I32),
                               in_=g_scale_rows[4 * quad:4 * quad + 4].bitcast(I32))
         load_g(0)
-        nc.sync.dma_start(out=a_raw0[1][:], in_=a_rows[0][:, 2:4, :])
-        load_u(0)
         load_g(1)
+        load_u(0, 0, 2)
         load_g(2)
-        load_u(1)
+        load_u(0, 2, 4)
         load_g(3)
+        load_u(1, 0, PACK)
         nc.sync.dma_start(out=a_raw1[:], in_=a_rows[1])
-        load_u(2)
-        load_u(3)
+        load_u(2, 0, PACK)
+        load_u(3, 0, PACK)
 
-        nc.scalar.activation(out=ln_mu_col[:], in_=mu_sb[:], func=ACT.Ln)
+        mu_bank = next_bank()
+        mu_words = mu_sb[:].bitcast(F32)
+        for e in range(2):
+            nc.tensor.transpose(mu_bank[:, e * P:(e + 1) * P], mu_words[:, e:e + 1].to_broadcast([P, P]), ident[:])
         for b in range(NB):
             nc.vector.tensor_scalar(out=row_rate[:, :, b, :], in0=lam_sb[:, :, 0:PACK], scalar1=kappa_sb[:, b:b + 1],
                                     scalar2=None, op0=ALU.add)
         nc.scalar.activation(out=ln_row[:].rearrange("p g b t -> p (g b t)"),
                              in_=row_rate[:].rearrange("p g b t -> p (g b t)"), func=ACT.Ln)
+        nc.scalar.activation(out=ln_mu[:].rearrange("p (n e h) -> p n e h", e=2, h=2),
+                             in_=mu_bank[:, 0:2 * P].bitcast(BF16).rearrange("p (e n h) -> p n e h", e=2, h=2), func=ACT.Ln)
+        natural = (0, 1, 2, 3)
+        first_last = (1, 2, 3, 0)
+
+        shares(0, (0, 1))
+        shares(1, (0, 1))
+        shares(0, (2, 3))
+        shares(1, (2, 3))
+        shares(2, first_last)
+        shares(3, first_last)
+        for t in range(PACK):
+            turn_a(0, t)
+        group_a(0, 0, nc.vector.tensor_copy)
         nc.vector.reciprocal(out=inv_row[:].rearrange("p g b t -> p (g b t)"),
                              in_=row_rate[:].rearrange("p g b t -> p (g b t)"))
-        mu_bank = next_bank()
-        for t in range(PACK):
-            nc.tensor.transpose(mu_bank[:, t * P:(t + 1) * P], ln_mu_col[:, t:t + 1].to_broadcast([P, P]), ident[:])
-        nc.vector.tensor_copy(out=ln_mu[:].rearrange("p (n t) -> p n t", t=PACK),
-                              in_=mu_bank[:].rearrange("p (t n) -> p n t", t=PACK))
-        shares(0)
-        shares(1)
-        shares(2)
-
-        turn_a(0, 0)
-        turn_a(0, 1)
-        group_a(0, 0, nc.vector.tensor_copy)
         group_a(0, 1, nc.vector.tensor_copy)
-        quantize_a(0, 0)
-        quantize_a(0, 1)
-        product(0, 0)
-        turn_a(0, 2)
-        product(0, 1)
-        turn_a(0, 3)
-        divide(0, 0)
+        quantize_a(0, 0, 0, 2)
         group_a(0, 2, nc.vector.tensor_copy)
-        divide(0, 1)
         group_a(0, 3, nc.vector.tensor_copy)
-        quantize_a(0, 2)
-        quantize_a(0, 3)
-        product(0, 2)
-        product(0, 3)
-        add_u(0, 0, 2, 0, NY)
-        divide(0, 2)
-        divide(0, 3)
-        for t in range(PACK):
-            product(1, t)
-        divide(1, 0)
-        add_u(0, 2, 4, 0, NY)
-        store_y(0, 0, NY)
+        quantize_a(0, 1, 0, 2)
+        first_pair = ((0, 0), (0, 1), (1, 0), (1, 1), (0, 2), (0, 3), (1, 2), (1, 3))
+        for k, t in first_pair:
+            product(k, t)
+        for n, (k, t) in enumerate(first_pair):
+            divide(k, t)
+            if n < 3:
+                add_u(nc.gpsimd, k, t, t + 1, 0, NY)
+        for t in first_last:
+            product(2, t)
+        for t in first_last:
+            product(3, t)
+        add_u(nc.vector, 0, 2, 4, 0, NY)
+        store_y(0, 0, PACK, 0, NY)
+        shares(4, first_last[:2])
         group_y(0, 0, NY, nc.scalar.copy)
-        shares(3)
+        add_u(nc.vector, 1, 1, 4, 0, NY)
+        store_y(1, 0, PACK, 0, NY)
+        group_y(1, 0, NY, nc.scalar.copy)
 
-        last = TILES - 1
-        for k in range(1, TILES):
-            for t in range(PACK):
-                if (k, t) != (1, 0):
-                    divide(k, t)
-                if k < last:
-                    product(k + 1, t)
-            if k == 1:
-                for t in range(PACK):
-                    turn_a(1, t)
-            add_u(k, 0, 2, 0, NY)
-            quantize_y(k - 1, 0, NY)
-            store_codes(k - 1, 0, NY)
-            if k - 1 == NB - 1:
-                store_scales(0, 0, NB * NY, [nc.sync] * 4)
-            if k - 1 == NB + 1:
-                store_scales(1, 0, 2 * NY, [nc.sync] * 4)
-            if k < last:
-                add_u(k, 2, 4, 0, NY)
-                store_y(k, 0, NY)
-                group_y(k, 0, NY, nc.scalar.copy)
-                if k == 1:
-                    for t in range(PACK):
-                        group_a(1, t, nc.scalar.copy)
-                elif k + 2 < TILES:
-                    shares(k + 2)
+        for k in range(2, TILES, 2):
+            more = k + 2 < TILES
+            for t in natural:
+                divide(k, t)
+                if t == 0:
+                    add_u(nc.gpsimd, k, 0, 1, 0, NY)
+                if t == 2:
+                    add_u(nc.gpsimd, k, 1, 3, 0, NY)
             if k == 2:
                 for t in range(PACK):
-                    quantize_a(1, t)
+                    turn_a(1, t)
+                    group_a(1, t, nc.scalar.copy)
+            if more:
+                shares(k + 2, first_last[2:] if k == 2 else first_last)
+            for t in natural:
+                divide(k + 1, t)
+            if k == 2:
+                quantize_a(1, 0, 0, 2)
+                quantize_y(0, 0, NY)
+                store_codes(0, 0, NY)
+                quantize_a(1, 1, 0, 2)
+            if more:
+                for t in first_last:
+                    product(k + 2, t)
+                for t in first_last:
+                    product(k + 3, t)
+            if not more:
+                store_y(k, 0, 1, 0, NY)
+                store_y(k, 1, 3, 0, NY)
+                quantize_y(k - 1, 0, NY)
+                store_codes(k - 1, 0, NY)
+            add_u(nc.vector, k, 3, 4, 0, NY)
+            group_y(k, 0, NY, nc.scalar.copy)
+            if more:
+                store_y(k, 0, PACK, 0, NY)
+                quantize_y(k - 1, 0, NY)
+                store_codes(k - 1, 0, NY)
+                if k == NB:
+                    store_scales(0, 0, NB * NY, [nc.sync] * 4)
+                shares(k + 3, first_last)
+                add_u(nc.vector, k + 1, 0, 4, 0, NY)
+                store_y(k + 1, 0, PACK, 0, NY)
+                group_y(k + 1, 0, NY, nc.scalar.copy)
+                quantize_y(k, 0, NY)
+                store_codes(k, 0, NY)
 
-        add_u(last, 2, 4, 0, HALF)
-        store_y(last, 0, HALF)
+        last = TILES - 1
+        store_y(last - 1, 3, 4, 0, NY)
+        add_u(nc.vector, last, 0, 4, 0, HALF)
+        store_y(last, 0, PACK, 0, HALF)
         group_y(last, 0, HALF, nc.scalar.copy)
-        add_u(last, 2, 4, HALF, NY)
-        store_y(last, HALF, NY)
+        add_u(nc.vector, last, 0, 4, HALF, NY)
+        store_y(last, 0, PACK, HALF, NY)
+        quantize_y(last - 1, 0, NY)
+        store_codes(last - 1, 0, NY)
         group_y(last, HALF, NY, nc.vector.tensor_copy)
         quantize_y(last, 0, HALF)
-        store_codes(last, 0, HALF)
         quantize_y(last, HALF, NY)
-        store_codes(last, HALF, NY)
-        store_scales(1, 2 * NY, NB * NY, [nc.sync, nc.sync, nc.scalar, nc.scalar])
+        store_codes(last, 0, NY)
+        store_scales(1, 0, NB * NY, [nc.sync, nc.sync, nc.scalar, nc.scalar])

@@ -56,9 +56,9 @@ def tile_second_side_rate_division_k2_kernel(tc, g_words, g_scales, a, lam, kapp
         mu_sb = kept("mu_sb", [P, PACK], BF16)
         lam_sb = kept("lam_sb", [P, GROUPS, 16], BF16)
         kappa_sb = kept("kappa_sb", [P, NB], BF16)
-        row_rate = kept("row_rate", [P, GROUPS, NB, PACK], F32)
-        ln_row = kept("ln_row", [P, GROUPS, NB, PACK], F32)
-        inv_row = kept("inv_row", [P, GROUPS, NB, PACK], F32)
+        row_rate = kept("row_rate", [P, NB, GROUPS, PACK], F32)
+        ln_row = kept("ln_row", [P, NB, GROUPS, PACK], F32)
+        inv_row = kept("inv_row", [P, NB, GROUPS, PACK], F32)
         ln_mu = kept("ln_mu", [P, NY], F32)
         g_plane = kept("g_plane", [P, PASSES, NB * NY], U8)
         g_codes = [kept("g_codes%d" % b, [P, PASSES, NY], U32) for b in range(NB)]
@@ -68,7 +68,8 @@ def tile_second_side_rate_division_k2_kernel(tc, g_words, g_scales, a, lam, kapp
         a_plane = {s: kept("a_plane%d%d" % s, [P, 2, PASSES * P], U8) for s in slots}
         a_grouped = {s: kept("a_grouped%d%d" % s, [P, 2, PASSES * P * PACK], BF16) for s in slots}
         u_sb = [kept("u_sb%d" % c, [P, PACK, 2 * NY], BF16) for c in range(TILES // 2)]
-        y_sb = [kept("y_sb%d" % c, [P, PACK, 2 * NY], F32) for c in range(TILES // 2)]
+        y_sb = [kept("y_sb%d" % k, [P, PACK, NY], F32) for k in range(TILES - 1)]
+        y_last = kept("y_last", [P, 2, PACK, HALF], F32)
         y_codes = [kept("y_codes%d" % k, [P, NY], U32) for k in range(TILES)]
         y_plane = [kept("y_plane%d" % g, [P, NB * NY], U8) for g in range(GROUPS)]
 
@@ -121,26 +122,30 @@ def tile_second_side_rate_division_k2_kernel(tc, g_words, g_scales, a, lam, kapp
                 share[k] = ring.tile([P, PACK, NY], F32, name="share%d" % k, tag="share", align_bytes=64)
             for t in ts:
                 nc.scalar.activation(out=share[k][:, t, :], in_=ln_mu[:], func=ACT.Sigmoid,
-                                     scale=-1.0, bias=ln_row[:, g, b, t:t + 1])
+                                     scale=-1.0, bias=ln_row[:, b, g, t:t + 1])
 
-        def y_tile(k):
-            return y_sb[k // 2][:, :, (k % 2) * NY:(k % 2 + 1) * NY]
+        def y_part(k, t0, t1, j0, j1):
+            if k == TILES - 1:
+                return y_last[:, j0 // HALF, t0:t1, :]
+            return y_sb[k][:, t0:t1, j0:j1]
 
-        def divide(k, t):
+        def divide(k, t, j0, j1):
             g, b = divmod(k, NB)
-            nc.vector.scalar_tensor_tensor(out=y_tile(k)[:, t, :], in0=h_bank[k, t][:], scalar=inv_row[:, g, b, t:t + 1],
-                                           in1=share[k][:, t, :], op0=ALU.mult, op1=ALU.mult)
+            nc.vector.scalar_tensor_tensor(out=y_part(k, t, t + 1, j0, j1)[:, 0, :], in0=h_bank[k, t][:, j0:j1],
+                                           scalar=inv_row[:, b, g, t:t + 1], in1=share[k][:, t, j0:j1],
+                                           op0=ALU.mult, op1=ALU.mult)
 
         def add_u(engine, k, t0, t1, j0, j1):
             off = (k % 2) * NY
-            engine.tensor_tensor(out=y_tile(k)[:, t0:t1, j0:j1], in0=y_tile(k)[:, t0:t1, j0:j1],
+            engine.tensor_tensor(out=y_part(k, t0, t1, j0, j1), in0=y_part(k, t0, t1, j0, j1),
                                  in1=u_sb[k // 2][:, t0:t1, off + j0:off + j1], op=ALU.add)
 
-        def group_y(k, j0, j1, copy):
-            tile_y = ring.tile([P, (j1 - j0) * PACK], BF16, name="y_grouped%d_%d" % (k, j0), tag="y_grouped", align_bytes=64)
-            y_grouped[k, j0] = tile_y
-            copy(out=tile_y[:].rearrange("p (c i t) -> p c t i", i=4, t=PACK),
-                 in_=y_tile(k)[:, :, j0:j1].rearrange("p t (c i) -> p c t i", i=4))
+        def group_y(k, j0, j1, c0, c1, copy):
+            if (k, j0) not in y_grouped:
+                y_grouped[k, j0] = ring.tile([P, (j1 - j0) * PACK], BF16, name="y_grouped%d_%d" % (k, j0),
+                                             tag="y_grouped", align_bytes=64)
+            copy(out=y_grouped[k, j0][:, c0 * PACK:c1 * PACK].rearrange("p (c i t) -> p c t i", i=4, t=PACK),
+                 in_=y_part(k, 0, PACK, j0, j1)[:, :, c0:c1].rearrange("p t (c i) -> p c t i", i=4))
 
         def quantize_y(k, j0, j1):
             g, b = divmod(k, NB)
@@ -149,7 +154,7 @@ def tile_second_side_rate_division_k2_kernel(tc, g_words, g_scales, a, lam, kapp
 
         def store_y(k, t0, t1, j0, j1):
             g, b = divmod(k, NB)
-            nc.sync.dma_start(out=y_rows[g][:, t0:t1, b, j0:j1], in_=y_tile(k)[:, t0:t1, j0:j1])
+            nc.sync.dma_start(out=y_rows[g][:, t0:t1, b, j0:j1], in_=y_part(k, t0, t1, j0, j1))
 
         def store_codes(k, j0, j1):
             g, b = divmod(k, NB)
@@ -188,10 +193,10 @@ def tile_second_side_rate_division_k2_kernel(tc, g_words, g_scales, a, lam, kapp
         for e in range(2):
             nc.tensor.transpose(mu_bank[:, e * P:(e + 1) * P], mu_words[:, e:e + 1].to_broadcast([P, P]), ident[:])
         for b in range(NB):
-            nc.vector.tensor_scalar(out=row_rate[:, :, b, :], in0=lam_sb[:, :, 0:PACK], scalar1=kappa_sb[:, b:b + 1],
+            nc.vector.tensor_scalar(out=row_rate[:, b, :, :], in0=lam_sb[:, :, 0:PACK], scalar1=kappa_sb[:, b:b + 1],
                                     scalar2=None, op0=ALU.add)
-        nc.scalar.activation(out=ln_row[:].rearrange("p g b t -> p (g b t)"),
-                             in_=row_rate[:].rearrange("p g b t -> p (g b t)"), func=ACT.Ln)
+        nc.scalar.activation(out=ln_row[:].rearrange("p b g t -> p (b g t)"),
+                             in_=row_rate[:].rearrange("p b g t -> p (b g t)"), func=ACT.Ln)
         nc.scalar.activation(out=ln_mu[:].rearrange("p (n e h) -> p n e h", e=2, h=2),
                              in_=mu_bank[:, 0:2 * P].bitcast(BF16).rearrange("p (e n h) -> p n e h", e=2, h=2), func=ACT.Ln)
         natural = (0, 1, 2, 3)
@@ -206,8 +211,8 @@ def tile_second_side_rate_division_k2_kernel(tc, g_words, g_scales, a, lam, kapp
         for t in range(PACK):
             turn_a(0, t)
         group_a(0, 0, nc.vector.tensor_copy)
-        nc.vector.reciprocal(out=inv_row[:].rearrange("p g b t -> p (g b t)"),
-                             in_=row_rate[:].rearrange("p g b t -> p (g b t)"))
+        nc.vector.reciprocal(out=inv_row[:].rearrange("p b g t -> p (b g t)"),
+                             in_=row_rate[:].rearrange("p b g t -> p (b g t)"))
         group_a(0, 1, nc.vector.tensor_copy)
         quantize_a(0, 0, 0, 2)
         group_a(0, 2, nc.vector.tensor_copy)
@@ -217,7 +222,7 @@ def tile_second_side_rate_division_k2_kernel(tc, g_words, g_scales, a, lam, kapp
         for k, t in first_pair:
             product(k, t)
         for n, (k, t) in enumerate(first_pair):
-            divide(k, t)
+            divide(k, t, 0, NY)
             if n < 3:
                 add_u(nc.gpsimd, k, t, t + 1, 0, NY)
         for t in first_last:
@@ -227,15 +232,15 @@ def tile_second_side_rate_division_k2_kernel(tc, g_words, g_scales, a, lam, kapp
         add_u(nc.vector, 0, 2, 4, 0, NY)
         store_y(0, 0, PACK, 0, NY)
         shares(4, first_last[:2])
-        group_y(0, 0, NY, nc.scalar.copy)
+        group_y(0, 0, NY, 0, NY, nc.scalar.copy)
         add_u(nc.vector, 1, 1, 4, 0, NY)
         store_y(1, 0, PACK, 0, NY)
-        group_y(1, 0, NY, nc.scalar.copy)
+        group_y(1, 0, NY, 0, NY, nc.scalar.copy)
 
         for k in range(2, TILES, 2):
             more = k + 2 < TILES
             for t in natural:
-                divide(k, t)
+                divide(k, t, 0, NY)
                 if t == 0:
                     add_u(nc.gpsimd, k, 0, 1, 0, NY)
                 if t == 2:
@@ -246,8 +251,9 @@ def tile_second_side_rate_division_k2_kernel(tc, g_words, g_scales, a, lam, kapp
                     group_a(1, t, nc.scalar.copy)
             if more:
                 shares(k + 2, first_last[2:] if k == 2 else first_last)
-            for t in natural:
-                divide(k + 1, t)
+            for j0, j1 in ((0, NY),) if more else ((0, HALF), (HALF, NY)):
+                for t in natural:
+                    divide(k + 1, t, j0, j1)
             if k == 2:
                 quantize_a(1, 0, 0, 2)
                 quantize_y(0, 0, NY)
@@ -261,10 +267,8 @@ def tile_second_side_rate_division_k2_kernel(tc, g_words, g_scales, a, lam, kapp
             if not more:
                 store_y(k, 0, 1, 0, NY)
                 store_y(k, 1, 3, 0, NY)
-                quantize_y(k - 1, 0, NY)
-                store_codes(k - 1, 0, NY)
             add_u(nc.vector, k, 3, 4, 0, NY)
-            group_y(k, 0, NY, nc.scalar.copy)
+            group_y(k, 0, NY, 0, NY, nc.scalar.copy)
             if more:
                 store_y(k, 0, PACK, 0, NY)
                 quantize_y(k - 1, 0, NY)
@@ -274,20 +278,23 @@ def tile_second_side_rate_division_k2_kernel(tc, g_words, g_scales, a, lam, kapp
                 shares(k + 3, first_last)
                 add_u(nc.vector, k + 1, 0, 4, 0, NY)
                 store_y(k + 1, 0, PACK, 0, NY)
-                group_y(k + 1, 0, NY, nc.scalar.copy)
+                group_y(k + 1, 0, NY, 0, NY, nc.scalar.copy)
                 quantize_y(k, 0, NY)
                 store_codes(k, 0, NY)
 
         last = TILES - 1
         store_y(last - 1, 3, 4, 0, NY)
+        quantize_y(last - 2, 0, NY)
+        store_codes(last - 2, 0, NY)
         add_u(nc.vector, last, 0, 4, 0, HALF)
         store_y(last, 0, PACK, 0, HALF)
-        group_y(last, 0, HALF, nc.scalar.copy)
+        group_y(last, 0, HALF, 0, HALF, nc.scalar.copy)
         add_u(nc.vector, last, 0, 4, HALF, NY)
         store_y(last, 0, PACK, HALF, NY)
+        group_y(last, HALF, NY, HALF // 2, HALF, nc.scalar.copy)
         quantize_y(last - 1, 0, NY)
         store_codes(last - 1, 0, NY)
-        group_y(last, HALF, NY, nc.vector.tensor_copy)
+        group_y(last, HALF, NY, 0, HALF // 2, nc.vector.tensor_copy)
         quantize_y(last, 0, HALF)
         quantize_y(last, HALF, NY)
         store_codes(last, 0, NY)

@@ -21,9 +21,9 @@ PACK = 4
 GROUP = P * PACK
 PASSES = NX // GROUP
 GROUPS = NI // GROUP
-TILES = GROUPS * NB
+PAIRS = GROUPS * NB // 2
 BANKS = 8
-HALF = NY // 2
+CUT = 64
 
 
 def tile_second_side_rate_division_k2_kernel(tc, g_words, g_scales, a, lam, kappa, mu, u, out_0, out_1, out_2):
@@ -46,7 +46,7 @@ def tile_second_side_rate_division_k2_kernel(tc, g_words, g_scales, a, lam, kapp
 
         slots = [(g, h) for g in range(GROUPS) for h in range(2)]
         a_rows = a.rearrange("(g m t) x -> g m t x", g=GROUPS, t=PACK)
-        u_rows = u.rearrange("(g p t) b j -> g p t (b j)", g=GROUPS, t=PACK)
+        u_rows = u.rearrange("(g p t) b j -> g p t b j", g=GROUPS, t=PACK)
         y_rows = out_0.rearrange("(g p t) b j -> g p t b j", g=GROUPS, t=PACK)
         g_cols = g_words.rearrange("q p n t -> p q (n t)")
         g_scale_rows = g_scales.rearrange("q r n -> r q n")
@@ -60,28 +60,46 @@ def tile_second_side_rate_division_k2_kernel(tc, g_words, g_scales, a, lam, kapp
         ln_row = kept("ln_row", [P, NB, GROUPS, PACK], F32)
         inv_row = kept("inv_row", [P, NB, GROUPS, PACK], F32)
         ln_mu = kept("ln_mu", [P, NY], F32)
-        g_plane = kept("g_plane", [P, PASSES, NB * NY], U8)
-        g_codes = [kept("g_codes%d" % b, [P, PASSES, NY], U32) for b in range(NB)]
+        g_plane = [kept("g_plane%d" % h, [P, PASSES, 2 * NY], U8) for h in range(2)]
+        g_codes = [kept("g_codes%d" % h, [P, PASSES, 2 * NY], U32) for h in range(2)]
+        g_first = kept("g_first", [P, PASSES, NY], U32)
         a_raw0 = [kept("a_raw0_%d" % h, [P, 2, NX], BF16) for h in range(2)]
         a_raw1 = kept("a_raw1", [P, PACK, NX], BF16)
         a_codes = {s: kept("a_codes%d%d" % s, [P, 2, PASSES * P], U32) for s in slots}
         a_plane = {s: kept("a_plane%d%d" % s, [P, 2, PASSES * P], U8) for s in slots}
         a_grouped = {s: kept("a_grouped%d%d" % s, [P, 2, PASSES * P * PACK], BF16) for s in slots}
-        u_sb = [kept("u_sb%d" % c, [P, PACK, 2 * NY], BF16) for c in range(TILES // 2)]
-        y_sb = [kept("y_sb%d" % k, [P, PACK, NY], F32) for k in range(TILES - 1)]
-        y_last = kept("y_last", [P, 2, PACK, HALF], F32)
-        y_codes = [kept("y_codes%d" % k, [P, NY], U32) for k in range(TILES)]
-        y_plane = [kept("y_plane%d" % g, [P, NB * NY], U8) for g in range(GROUPS)]
+        u_first = [kept("u_first%d" % h, [P, PACK, 2, NY], BF16) for h in range(2)]
+        u_second = kept("u_second", [P, PACK, NB, NY], BF16)
+        y_pair = [kept("y_pair%d" % c, [P, PACK, 2, NY], F32) for c in range(PAIRS - 1)]
+        y_last = [kept("y_last%d" % s, [P, PACK, NY], F32) for s in range(2)]
+        y_codes = [kept("y_codes%d" % c, [P, 2 * NY], U32) for c in range(PAIRS)]
+        y_plane = [kept("y_plane%d" % g, [P, NY], U8) for g in range(GROUPS)]
 
-        a_bank, h_bank, share, y_grouped = {}, {}, {}, {}
+        a_bank, h_bank, share, share_tiles, y_grouped = {}, {}, {}, {}, {}
 
-        def load_g(b):
-            nc.sync.dma_start(out=g_codes[b][:].bitcast(I32),
-                              in_=g_cols[:, :, b * NY * PACK:(b + 1) * NY * PACK].bitcast(I32))
+        def load_g(dest, b0, b1):
+            nc.sync.dma_start(out=dest.bitcast(I32), in_=g_cols[:, :, b0 * NY * PACK:b1 * NY * PACK].bitcast(I32))
 
-        def load_u(c, t0, t1):
+        def load_g_scales(h):
+            for quad in range(4):
+                nc.sync.dma_start(out=g_plane[h][32 * quad:32 * quad + 4, :, :].bitcast(I32),
+                                  in_=g_scale_rows[4 * quad:4 * quad + 4, :, h * 2 * NY:(h + 1) * 2 * NY].bitcast(I32))
+
+        def g_tile(b, q):
+            if b == 0:
+                return g_first[:, q, :]
+            return g_codes[b // 2][:, q, (b % 2) * NY:(b % 2 + 1) * NY]
+
+        def u_part(c, t0, t1, s0, s1):
             g, h = divmod(c, 2)
-            nc.sync.dma_start(out=u_sb[c][:, t0:t1, :], in_=u_rows[g][:, t0:t1, h * 2 * NY:(h + 1) * 2 * NY])
+            if g == 0:
+                return u_first[h][:, t0:t1, s0:s1, :]
+            return u_second[:, t0:t1, 2 * h + s0:2 * h + s1, :]
+
+        def y_part(c, t0, t1, s0, s1):
+            if c == PAIRS - 1:
+                return y_last[s0][:, t0:t1, :].unsqueeze(2)
+            return y_pair[c][:, t0:t1, s0:s1, :]
 
         def turn_a(g, t):
             raw = a_raw0[t // 2][:, t % 2, :] if g == 0 else a_raw1[:, t, :]
@@ -103,70 +121,81 @@ def tile_second_side_rate_division_k2_kernel(tc, g_words, g_scales, a, lam, kapp
                                   scales=a_plane[g, h][:, s0:s1, :].rearrange("p s n -> p (s n)"),
                                   in_=a_grouped[g, h][:, s0:s1, :].rearrange("p s n -> p (s n)"))
 
-        def product(k, t):
-            g, b = divmod(k, NB)
+        def product(c, t, s):
+            g, h = divmod(c, 2)
             bank = next_bank()
-            h_bank[k, t] = bank
+            h_bank[c, t, s] = bank
             for q in range(PASSES):
                 nc.tensor.matmul_mx(
                     out=bank[:],
                     lhsT=a_codes[g, t // 2][:, t % 2, q * P:(q + 1) * P].bitcast(E4M3),
                     lhsT_scale=a_plane[g, t // 2][:, t % 2, q * P:(q + 1) * P],
-                    rhs=g_codes[b][:, q, :].bitcast(E5M2),
-                    rhs_scale=g_plane[:, q, b * NY:(b + 1) * NY],
+                    rhs=g_tile(2 * h + s, q).bitcast(E5M2),
+                    rhs_scale=g_plane[h][:, q, s * NY:(s + 1) * NY],
                     start=(q == 0), stop=(q == PASSES - 1))
 
-        def shares(k, ts):
-            g, b = divmod(k, NB)
-            if k not in share:
-                share[k] = ring.tile([P, PACK, NY], F32, name="share%d" % k, tag="share", align_bytes=64)
-            for t in ts:
-                nc.scalar.activation(out=share[k][:, t, :], in_=ln_mu[:], func=ACT.Sigmoid,
-                                     scale=-1.0, bias=ln_row[:, b, g, t:t + 1])
+        def parts(c):
+            if c == PAIRS - 1:
+                return [(t, s) for s in range(2) for t in range(PACK)]
+            return [(t, s) for t in range(PACK) for s in range(2)]
 
-        def y_part(k, t0, t1, j0, j1):
-            if k == TILES - 1:
-                return y_last[:, j0 // HALF, t0:t1, :]
-            return y_sb[k][:, t0:t1, j0:j1]
+        def made_order(c):
+            return range(8) if c == 0 else (1, 2, 3, 0, 5, 6, 7, 4)
 
-        def divide(k, t, j0, j1):
-            g, b = divmod(k, NB)
-            nc.vector.scalar_tensor_tensor(out=y_part(k, t, t + 1, j0, j1)[:, 0, :], in0=h_bank[k, t][:, j0:j1],
-                                           scalar=inv_row[:, b, g, t:t + 1], in1=share[k][:, t, j0:j1],
+        def products(c, n0, n1):
+            for n in made_order(c)[n0:n1]:
+                product(c, *parts(c)[n])
+
+        def shares(c, n0, n1):
+            g, h = divmod(c, 2)
+            for n in made_order(c)[n0:n1]:
+                t, s = parts(c)[n]
+                if (c, n // 4) not in share_tiles:
+                    share_tiles[c, n // 4] = ring.tile([P, 4, NY], F32, name="share%d_%d" % (c, n // 4), tag="share",
+                                                       align_bytes=64)
+                share[c, t, s] = share_tiles[c, n // 4][:, n % 4, :]
+                nc.scalar.activation(out=share[c, t, s], in_=ln_mu[:], func=ACT.Sigmoid,
+                                     scale=-1.0, bias=ln_row[:, 2 * h + s, g, t:t + 1])
+
+        def divide(c, t, s):
+            g, h = divmod(c, 2)
+            nc.vector.scalar_tensor_tensor(out=y_part(c, t, t + 1, s, s + 1)[:, 0, 0, :], in0=h_bank[c, t, s][:],
+                                           scalar=inv_row[:, 2 * h + s, g, t:t + 1], in1=share[c, t, s],
                                            op0=ALU.mult, op1=ALU.mult)
 
-        def add_u(engine, k, t0, t1, j0, j1):
-            off = (k % 2) * NY
-            engine.tensor_tensor(out=y_part(k, t0, t1, j0, j1), in0=y_part(k, t0, t1, j0, j1),
-                                 in1=u_sb[k // 2][:, t0:t1, off + j0:off + j1], op=ALU.add)
+        def add_u(engine, c, t0, t1, s0, s1):
+            engine.tensor_tensor(out=y_part(c, t0, t1, s0, s1), in0=y_part(c, t0, t1, s0, s1),
+                                 in1=u_part(c, t0, t1, s0, s1), op=ALU.add)
 
-        def group_y(k, j0, j1, c0, c1, copy):
-            if (k, j0) not in y_grouped:
-                y_grouped[k, j0] = ring.tile([P, (j1 - j0) * PACK], BF16, name="y_grouped%d_%d" % (k, j0),
-                                             tag="y_grouped", align_bytes=64)
-            copy(out=y_grouped[k, j0][:, c0 * PACK:c1 * PACK].rearrange("p (c i t) -> p c t i", i=4, t=PACK),
-                 in_=y_part(k, 0, PACK, j0, j1)[:, :, c0:c1].rearrange("p t (c i) -> p c t i", i=4))
+        def group_y(c, s, j0, j1, copy):
+            if (c, s) not in y_grouped:
+                y_grouped[c, s] = ring.tile([P, NY * PACK], BF16, name="y_grouped%d_%d" % (c, s),
+                                            tag="y_grouped", align_bytes=64)
+            copy(out=y_grouped[c, s][:, j0 * PACK:j1 * PACK].rearrange("p (c i t) -> p c t i", i=4, t=PACK),
+                 in_=y_part(c, 0, PACK, s, s + 1)[:, :, 0, j0:j1].rearrange("p t (c i) -> p c t i", i=4))
 
-        def quantize_y(k, j0, j1):
-            g, b = divmod(k, NB)
-            nc.vector.quantize_mx(out=y_codes[k][:, j0:j1].bitcast(E4M3),
-                                  scales=y_plane[g][:, b * NY + j0:b * NY + j1], in_=y_grouped[k, j0][:])
+        def quantize_y(c, s):
+            g, h = divmod(c, 2)
+            b = 2 * h + s
+            nc.vector.quantize_mx(out=y_codes[c][:, s * NY:(s + 1) * NY].bitcast(E4M3),
+                                  scales=y_plane[g][4 * b:P, :], in_=y_grouped[c, s][:])
 
-        def store_y(k, t0, t1, j0, j1):
-            g, b = divmod(k, NB)
-            nc.sync.dma_start(out=y_rows[g][:, t0:t1, b, j0:j1], in_=y_part(k, t0, t1, j0, j1))
+        def store_y(c, t0, t1, s0, s1):
+            g, h = divmod(c, 2)
+            nc.sync.dma_start(out=y_rows[g][:, t0:t1, 2 * h + s0:2 * h + s1, :], in_=y_part(c, t0, t1, s0, s1))
 
-        def store_codes(k, j0, j1):
-            g, b = divmod(k, NB)
-            c0, c1 = (b * NY + j0) * PACK, (b * NY + j1) * PACK
-            nc.sync.dma_start(out=y_words_out[g][:, c0:c1].bitcast(I32), in_=y_codes[k][:, j0:j1].bitcast(I32))
+        def store_codes(c, s0, s1):
+            g, h = divmod(c, 2)
+            c0, c1 = (2 * h + s0) * NY * PACK, (2 * h + s1) * NY * PACK
+            nc.sync.dma_start(out=y_words_out[g][:, c0:c1].bitcast(I32), in_=y_codes[c][:, s0 * NY:s1 * NY].bitcast(I32))
 
-        def store_scales(g, c0, c1, queues):
+        def store_scales(g, queues):
             for quad in range(4):
-                queues[quad].dma_start(out=out_2[g][4 * quad:4 * quad + 4, c0:c1].bitcast(I32),
-                                       in_=y_plane[g][32 * quad:32 * quad + 4, c0:c1].bitcast(I32))
+                queues[quad].dma_start(out=out_2[g][4 * quad:4 * quad + 4, :].bitcast(I32).rearrange("r (b j) -> b r j", b=NB),
+                                       in_=y_plane[g][32 * quad:32 * quad + 16, :].bitcast(I32))
 
-        nc.vector.memset(g_plane[:].rearrange("p q n -> p (q n)").bitcast(I32), 0)
+        for h in range(2):
+            nc.vector.memset(g_plane[h][:].rearrange("p q n -> p (q n)").bitcast(I32), 0)
         make_identity(nc, ident[:])
         nc.sync.dma_start(out=mu_sb[:], in_=mu.rearrange("(p t) -> p t", t=PACK))
         nc.sync.dma_start(out=lam_sb[:, :, 0:PACK], in_=lam.rearrange("(g p t) -> p g t", g=GROUPS, t=PACK))
@@ -174,19 +203,16 @@ def tile_second_side_rate_division_k2_kernel(tc, g_words, g_scales, a, lam, kapp
         nc.sync.dma_start(out=a_raw0[0][:, 0, :], in_=a_rows[0][:, 0, :])
         nc.sync.dma_start(out=a_raw0[0][:, 1, :], in_=a_rows[0][:, 1, :])
         nc.sync.dma_start(out=a_raw0[1][:], in_=a_rows[0][:, 2:4, :])
-        for quad in range(4):
-            nc.sync.dma_start(out=g_plane[32 * quad:32 * quad + 4, :, :].bitcast(I32),
-                              in_=g_scale_rows[4 * quad:4 * quad + 4].bitcast(I32))
-        load_g(0)
-        load_g(1)
-        load_u(0, 0, 2)
-        load_g(2)
-        load_u(0, 2, 4)
-        load_g(3)
-        load_u(1, 0, PACK)
+        load_g_scales(0)
+        load_g(g_first[:], 0, 1)
+        load_g(g_codes[0][:, :, NY:2 * NY], 1, 2)
+        nc.sync.dma_start(out=u_first[0][:, 0:2], in_=u_rows[0][:, 0:2, 0:2, :])
+        load_g_scales(1)
+        nc.sync.dma_start(out=u_first[0][:, 2:4], in_=u_rows[0][:, 2:4, 0:2, :])
+        load_g(g_codes[1][:], 2, 4)
+        nc.sync.dma_start(out=u_first[1][:], in_=u_rows[0][:, :, 2:4, :])
         nc.sync.dma_start(out=a_raw1[:], in_=a_rows[1])
-        load_u(2, 0, PACK)
-        load_u(3, 0, PACK)
+        nc.sync.dma_start(out=u_second[:], in_=u_rows[1])
 
         mu_bank = next_bank()
         mu_words = mu_sb[:].bitcast(F32)
@@ -199,15 +225,9 @@ def tile_second_side_rate_division_k2_kernel(tc, g_words, g_scales, a, lam, kapp
                              in_=row_rate[:].rearrange("p b g t -> p (b g t)"), func=ACT.Ln)
         nc.scalar.activation(out=ln_mu[:].rearrange("p (n e h) -> p n e h", e=2, h=2),
                              in_=mu_bank[:, 0:2 * P].bitcast(BF16).rearrange("p (e n h) -> p n e h", e=2, h=2), func=ACT.Ln)
-        natural = (0, 1, 2, 3)
-        first_last = (1, 2, 3, 0)
 
-        shares(0, (0, 1))
-        shares(1, (0, 1))
-        shares(0, (2, 3))
-        shares(1, (2, 3))
-        shares(2, first_last)
-        shares(3, first_last)
+        shares(0, 0, 8)
+        shares(1, 0, 8)
         for t in range(PACK):
             turn_a(0, t)
         group_a(0, 0, nc.vector.tensor_copy)
@@ -218,84 +238,80 @@ def tile_second_side_rate_division_k2_kernel(tc, g_words, g_scales, a, lam, kapp
         group_a(0, 2, nc.vector.tensor_copy)
         group_a(0, 3, nc.vector.tensor_copy)
         quantize_a(0, 1, 0, 2)
-        first_pair = ((0, 0), (0, 1), (1, 0), (1, 1), (0, 2), (0, 3), (1, 2), (1, 3))
-        for k, t in first_pair:
-            product(k, t)
-        for n, (k, t) in enumerate(first_pair):
-            divide(k, t, 0, NY)
-            if n < 3:
-                add_u(nc.gpsimd, k, t, t + 1, 0, NY)
-        for t in first_last:
-            product(2, t)
-        for t in first_last:
-            product(3, t)
-        add_u(nc.vector, 0, 2, 4, 0, NY)
-        store_y(0, 0, PACK, 0, NY)
-        shares(4, first_last[:2])
-        group_y(0, 0, NY, 0, NY, nc.scalar.copy)
-        add_u(nc.vector, 1, 1, 4, 0, NY)
-        store_y(1, 0, PACK, 0, NY)
-        group_y(1, 0, NY, 0, NY, nc.scalar.copy)
+        products(0, 0, 8)
 
-        for k in range(2, TILES, 2):
-            more = k + 2 < TILES
-            for t in natural:
-                divide(k, t, 0, NY)
-                if t == 0:
-                    add_u(nc.gpsimd, k, 0, 1, 0, NY)
-                if t == 2:
-                    add_u(nc.gpsimd, k, 1, 3, 0, NY)
-            if k == 2:
-                for t in range(PACK):
-                    turn_a(1, t)
-                    group_a(1, t, nc.scalar.copy)
-            if more:
-                shares(k + 2, first_last[2:] if k == 2 else first_last)
-            for j0, j1 in ((0, NY),) if more else ((0, HALF), (HALF, NY)):
-                for t in natural:
-                    divide(k + 1, t, j0, j1)
-            if k == 2:
-                quantize_a(1, 0, 0, 2)
-                quantize_y(0, 0, NY)
-                store_codes(0, 0, NY)
-                quantize_a(1, 1, 0, 2)
-            if more:
-                for t in first_last:
-                    product(k + 2, t)
-                for t in first_last:
-                    product(k + 3, t)
-            if not more:
-                store_y(k, 0, 1, 0, NY)
-                store_y(k, 1, 3, 0, NY)
-            add_u(nc.vector, k, 3, 4, 0, NY)
-            group_y(k, 0, NY, 0, NY, nc.scalar.copy)
-            if more:
-                store_y(k, 0, PACK, 0, NY)
-                quantize_y(k - 1, 0, NY)
-                store_codes(k - 1, 0, NY)
-                if k == NB:
-                    store_scales(0, 0, NB * NY, [nc.sync] * 4)
-                shares(k + 3, first_last)
-                add_u(nc.vector, k + 1, 0, 4, 0, NY)
-                store_y(k + 1, 0, PACK, 0, NY)
-                group_y(k + 1, 0, NY, 0, NY, nc.scalar.copy)
-                quantize_y(k, 0, NY)
-                store_codes(k, 0, NY)
+        def divide_pair(c, n0, n1):
+            for n in range(n0, n1):
+                t, s = parts(c)[n]
+                divide(c, t, s)
+                if n < 3:
+                    add_u(nc.gpsimd, c, t, t + 1, s, s + 1)
 
-        last = TILES - 1
-        store_y(last - 1, 3, 4, 0, NY)
-        quantize_y(last - 2, 0, NY)
-        store_codes(last - 2, 0, NY)
-        add_u(nc.vector, last, 0, 4, 0, HALF)
-        store_y(last, 0, PACK, 0, HALF)
-        group_y(last, 0, HALF, 0, HALF, nc.scalar.copy)
-        add_u(nc.vector, last, 0, 4, HALF, NY)
-        store_y(last, 0, PACK, HALF, NY)
-        group_y(last, HALF, NY, HALF // 2, HALF, nc.scalar.copy)
-        quantize_y(last - 1, 0, NY)
-        store_codes(last - 1, 0, NY)
-        group_y(last, HALF, NY, 0, HALF // 2, nc.vector.tensor_copy)
-        quantize_y(last, 0, HALF)
-        quantize_y(last, HALF, NY)
-        store_codes(last, 0, NY)
-        store_scales(1, 0, NB * NY, [nc.sync, nc.sync, nc.scalar, nc.scalar])
+        def finish_pair(c, t0, t1, s0):
+            add_u(nc.vector, c, max(t0, 1), t1, s0, 2)
+            store_y(c, t0, t1, 0, 2)
+
+        last = PAIRS - 1
+        divide_pair(0, 0, 8)
+        products(1, 0, 8)
+        shares(2, 0, 5)
+        finish_pair(0, 0, 2, 1)
+        finish_pair(0, 2, 4, 0)
+        group_y(0, 0, 0, NY, nc.scalar.copy)
+
+        divide_pair(1, 0, 4)
+        for slot in range(PACK):
+            turn_a(1, slot)
+            group_a(1, slot, nc.scalar.copy)
+        group_y(0, 1, 0, NY, nc.scalar.copy)
+        shares(2, 5, 8)
+        divide_pair(1, 4, 8)
+        quantize_a(1, 0, 0, 2)
+        products(2, 0, 4)
+        finish_pair(1, 0, 2, 1)
+        quantize_y(0, 0)
+        finish_pair(1, 2, 4, 0)
+        quantize_a(1, 1, 0, 2)
+        products(2, 4, 8)
+        quantize_y(0, 1)
+        store_codes(0, 0, 2)
+        group_y(1, 0, 0, NY, nc.scalar.copy)
+        group_y(1, 1, 0, NY, nc.scalar.copy)
+        shares(3, 0, 8)
+
+        divide_pair(2, 0, 8)
+        products(3, 0, 8)
+        quantize_y(1, 0)
+        finish_pair(2, 0, 2, 1)
+        quantize_y(1, 1)
+        store_codes(1, 0, 2)
+        store_scales(0, [nc.sync] * 4)
+        finish_pair(2, 2, 4, 0)
+        group_y(2, 0, 0, NY, nc.scalar.copy)
+        group_y(2, 1, 0, NY, nc.scalar.copy)
+
+        for n, (t, s) in enumerate(parts(last)):
+            divide(last, t, s)
+            if n == 0:
+                add_u(nc.gpsimd, last, 0, 1, 0, 1)
+                store_y(last, 0, 1, 0, 1)
+            if n == 2:
+                add_u(nc.gpsimd, last, 1, 3, 0, 1)
+                store_y(last, 1, 3, 0, 1)
+        add_u(nc.vector, last, 3, 4, 0, 1)
+        store_y(last, 3, 4, 0, 1)
+        group_y(last, 0, 0, NY, nc.scalar.copy)
+        add_u(nc.vector, last, 0, 2, 1, 2)
+        store_y(last, 0, 2, 1, 2)
+        add_u(nc.vector, last, 2, 4, 1, 2)
+        store_y(last, 2, 4, 1, 2)
+        group_y(last, 1, CUT, NY, nc.scalar.copy)
+        quantize_y(last - 1, 0)
+        group_y(last, 1, 0, CUT, nc.vector.tensor_copy)
+        quantize_y(last - 1, 1)
+        store_codes(last - 1, 0, 2)
+        quantize_y(last, 0)
+        store_codes(last, 0, 1)
+        quantize_y(last, 1)
+        store_codes(last, 1, 2)
+        store_scales(1, [nc.sync, nc.sync, nc.scalar, nc.scalar])

from contextlib import ExitStack

import concourse.mybir as mybir
from concourse.masks import make_identity

NI, NX, NB, NY = 1024, 1024, 4, 512
FLOPS = 2 * NI * NX * NB * NY

F32 = mybir.dt.float32
BF16 = mybir.dt.bfloat16
I32 = mybir.dt.int32
U32 = mybir.dt.uint32
U8 = mybir.dt.uint8
E4M3 = mybir.dt.float8_e4m3fn_x4
E5M2 = mybir.dt.float8_e5m2_x4
ALU = mybir.AluOpType
ACT = mybir.ActivationFunctionType

P = 128
PACK = 4
GROUP = P * PACK
PASSES = NX // GROUP
GROUPS = NI // GROUP
PAIRS = GROUPS * NB // 2
BANKS = 8
CUT = 64


def tile_second_side_rate_division_k2_kernel(tc, g_words, g_scales, a, lam, kappa, mu, u, out_0, out_1, out_2):
    nc = tc.nc
    with ExitStack() as ctx:
        keep = ctx.enter_context(tc.tile_pool(name="keep", bufs=1))
        ring = ctx.enter_context(tc.tile_pool(name="ring", bufs=4))
        psum = ctx.enter_context(tc.psum_pool(name="psum", bufs=1))
        ctx.enter_context(tc.manual_schedule())

        banks_taken = []

        def next_bank():
            n = len(banks_taken)
            banks_taken.append(n)
            return psum.tile([P, NY], F32, name="bank%d" % n, tag="bank%d" % (n % BANKS))

        def kept(name, shape, dtype):
            return keep.tile(shape, dtype, name=name, tag=name, align_bytes=64)

        slots = [(g, h) for g in range(GROUPS) for h in range(2)]
        a_rows = a.rearrange("(g m t) x -> g m t x", g=GROUPS, t=PACK)
        u_rows = u.rearrange("(g p t) b j -> g p t b j", g=GROUPS, t=PACK)
        y_rows = out_0.rearrange("(g p t) b j -> g p t b j", g=GROUPS, t=PACK)
        g_cols = g_words.rearrange("q p n t -> p q (n t)")
        g_scale_rows = g_scales.rearrange("q r n -> r q n")
        y_words_out = out_1.rearrange("g p n t -> g p (n t)")

        ident = kept("ident", [P, P], F32)
        mu_sb = kept("mu_sb", [P, PACK], BF16)
        lam_sb = kept("lam_sb", [P, GROUPS, 16], BF16)
        kappa_sb = kept("kappa_sb", [P, NB], BF16)
        row_rate = kept("row_rate", [P, NB, GROUPS, PACK], F32)
        ln_row = kept("ln_row", [P, NB, GROUPS, PACK], F32)
        inv_row = kept("inv_row", [P, NB, GROUPS, PACK], F32)
        ln_mu = kept("ln_mu", [P, NY], F32)
        g_plane = [kept("g_plane%d" % h, [P, PASSES, 2 * NY], U8) for h in range(2)]
        g_codes = [kept("g_codes%d" % h, [P, PASSES, 2 * NY], U32) for h in range(2)]
        g_first = kept("g_first", [P, PASSES, NY], U32)
        a_raw0 = [kept("a_raw0_%d" % h, [P, 2, NX], BF16) for h in range(2)]
        a_raw1 = kept("a_raw1", [P, PACK, NX], BF16)
        a_codes = {s: kept("a_codes%d%d" % s, [P, 2, PASSES * P], U32) for s in slots}
        a_plane = {s: kept("a_plane%d%d" % s, [P, 2, PASSES * P], U8) for s in slots}
        a_grouped = {s: kept("a_grouped%d%d" % s, [P, 2, PASSES * P * PACK], BF16) for s in slots}
        u_first = [kept("u_first%d" % h, [P, PACK, 2, NY], BF16) for h in range(2)]
        u_second = kept("u_second", [P, PACK, NB, NY], BF16)
        y_pair = [kept("y_pair%d" % c, [P, PACK, 2, NY], F32) for c in range(PAIRS - 1)]
        y_last = [kept("y_last%d" % s, [P, PACK, NY], F32) for s in range(2)]
        y_codes = [kept("y_codes%d" % c, [P, 2 * NY], U32) for c in range(PAIRS)]
        y_plane = [kept("y_plane%d" % g, [P, NY], U8) for g in range(GROUPS)]

        a_bank, h_bank, share, share_tiles, y_grouped = {}, {}, {}, {}, {}

        def load_g(dest, b0, b1):
            nc.sync.dma_start(out=dest.bitcast(I32), in_=g_cols[:, :, b0 * NY * PACK:b1 * NY * PACK].bitcast(I32))

        def load_g_scales(h):
            for quad in range(4):
                nc.sync.dma_start(out=g_plane[h][32 * quad:32 * quad + 4, :, :].bitcast(I32),
                                  in_=g_scale_rows[4 * quad:4 * quad + 4, :, h * 2 * NY:(h + 1) * 2 * NY].bitcast(I32))

        def g_tile(b, q):
            if b == 0:
                return g_first[:, q, :]
            return g_codes[b // 2][:, q, (b % 2) * NY:(b % 2 + 1) * NY]

        def u_part(c, t0, t1, s0, s1):
            g, h = divmod(c, 2)
            if g == 0:
                return u_first[h][:, t0:t1, s0:s1, :]
            return u_second[:, t0:t1, 2 * h + s0:2 * h + s1, :]

        def y_part(c, t0, t1, s0, s1):
            if c == PAIRS - 1:
                return y_last[s0][:, t0:t1, :].unsqueeze(2)
            return y_pair[c][:, t0:t1, s0:s1, :]

        def turn_a(g, t):
            raw = a_raw0[t // 2][:, t % 2, :] if g == 0 else a_raw1[:, t, :]
            words = raw.bitcast(F32)
            bank = next_bank()
            a_bank[g, t] = bank
            for q in range(PASSES):
                for e in range(2):
                    n = 2 * q + e
                    nc.tensor.transpose(bank[:, n * P:(n + 1) * P],
                                        words[:, 2 * P * q + e:2 * P * (q + 1):2], ident[:])

        def group_a(g, t, copy):
            copy(out=a_grouped[g, t // 2][:, t % 2, :].bitcast(F32).rearrange("p (q m e) -> p q m e", q=PASSES, e=2),
                 in_=a_bank[g, t][:].rearrange("p (q e m) -> p q m e", q=PASSES, e=2))

        def quantize_a(g, h, s0, s1):
            nc.vector.quantize_mx(out=a_codes[g, h][:, s0:s1, :].rearrange("p s n -> p (s n)").bitcast(E4M3),
                                  scales=a_plane[g, h][:, s0:s1, :].rearrange("p s n -> p (s n)"),
                                  in_=a_grouped[g, h][:, s0:s1, :].rearrange("p s n -> p (s n)"))

        def product(c, t, s):
            g, h = divmod(c, 2)
            bank = next_bank()
            h_bank[c, t, s] = bank
            for q in range(PASSES):
                nc.tensor.matmul_mx(
                    out=bank[:],
                    lhsT=a_codes[g, t // 2][:, t % 2, q * P:(q + 1) * P].bitcast(E4M3),
                    lhsT_scale=a_plane[g, t // 2][:, t % 2, q * P:(q + 1) * P],
                    rhs=g_tile(2 * h + s, q).bitcast(E5M2),
                    rhs_scale=g_plane[h][:, q, s * NY:(s + 1) * NY],
                    start=(q == 0), stop=(q == PASSES - 1))

        def parts(c):
            if c == PAIRS - 1:
                return [(t, s) for s in range(2) for t in range(PACK)]
            return [(t, s) for t in range(PACK) for s in range(2)]

        def made_order(c):
            return range(8) if c == 0 else (1, 2, 3, 0, 5, 6, 7, 4)

        def products(c, n0, n1):
            for n in made_order(c)[n0:n1]:
                product(c, *parts(c)[n])

        def shares(c, n0, n1):
            g, h = divmod(c, 2)
            for n in made_order(c)[n0:n1]:
                t, s = parts(c)[n]
                if (c, n // 4) not in share_tiles:
                    share_tiles[c, n // 4] = ring.tile([P, 4, NY], F32, name="share%d_%d" % (c, n // 4), tag="share",
                                                       align_bytes=64)
                share[c, t, s] = share_tiles[c, n // 4][:, n % 4, :]
                nc.scalar.activation(out=share[c, t, s], in_=ln_mu[:], func=ACT.Sigmoid,
                                     scale=-1.0, bias=ln_row[:, 2 * h + s, g, t:t + 1])

        def divide(c, t, s):
            g, h = divmod(c, 2)
            nc.vector.scalar_tensor_tensor(out=y_part(c, t, t + 1, s, s + 1)[:, 0, 0, :], in0=h_bank[c, t, s][:],
                                           scalar=inv_row[:, 2 * h + s, g, t:t + 1], in1=share[c, t, s],
                                           op0=ALU.mult, op1=ALU.mult)

        def add_u(engine, c, t0, t1, s0, s1):
            engine.tensor_tensor(out=y_part(c, t0, t1, s0, s1), in0=y_part(c, t0, t1, s0, s1),
                                 in1=u_part(c, t0, t1, s0, s1), op=ALU.add)

        def group_y(c, s, j0, j1, copy):
            if (c, s) not in y_grouped:
                y_grouped[c, s] = ring.tile([P, NY * PACK], BF16, name="y_grouped%d_%d" % (c, s),
                                            tag="y_grouped", align_bytes=64)
            copy(out=y_grouped[c, s][:, j0 * PACK:j1 * PACK].rearrange("p (c i t) -> p c t i", i=4, t=PACK),
                 in_=y_part(c, 0, PACK, s, s + 1)[:, :, 0, j0:j1].rearrange("p t (c i) -> p c t i", i=4))

        def quantize_y(c, s):
            g, h = divmod(c, 2)
            b = 2 * h + s
            nc.vector.quantize_mx(out=y_codes[c][:, s * NY:(s + 1) * NY].bitcast(E4M3),
                                  scales=y_plane[g][4 * b:P, :], in_=y_grouped[c, s][:])

        def store_y(c, t0, t1, s0, s1):
            g, h = divmod(c, 2)
            nc.sync.dma_start(out=y_rows[g][:, t0:t1, 2 * h + s0:2 * h + s1, :], in_=y_part(c, t0, t1, s0, s1))

        def store_codes(c, s0, s1):
            g, h = divmod(c, 2)
            c0, c1 = (2 * h + s0) * NY * PACK, (2 * h + s1) * NY * PACK
            nc.sync.dma_start(out=y_words_out[g][:, c0:c1].bitcast(I32), in_=y_codes[c][:, s0 * NY:s1 * NY].bitcast(I32))

        def store_scales(g, queues):
            for quad in range(4):
                queues[quad].dma_start(out=out_2[g][4 * quad:4 * quad + 4, :].bitcast(I32).rearrange("r (b j) -> b r j", b=NB),
                                       in_=y_plane[g][32 * quad:32 * quad + 16, :].bitcast(I32))

        for h in range(2):
            nc.vector.memset(g_plane[h][:].rearrange("p q n -> p (q n)").bitcast(I32), 0)
        make_identity(nc, ident[:])
        nc.sync.dma_start(out=mu_sb[:], in_=mu.rearrange("(p t) -> p t", t=PACK))
        nc.sync.dma_start(out=lam_sb[:, :, 0:PACK], in_=lam.rearrange("(g p t) -> p g t", g=GROUPS, t=PACK))
        nc.sync.dma_start(out=kappa_sb[:], in_=kappa.partition_broadcast(P))
        nc.sync.dma_start(out=a_raw0[0][:, 0, :], in_=a_rows[0][:, 0, :])
        nc.sync.dma_start(out=a_raw0[0][:, 1, :], in_=a_rows[0][:, 1, :])
        nc.sync.dma_start(out=a_raw0[1][:], in_=a_rows[0][:, 2:4, :])
        load_g_scales(0)
        load_g(g_first[:], 0, 1)
        load_g(g_codes[0][:, :, NY:2 * NY], 1, 2)
        nc.sync.dma_start(out=u_first[0][:, 0:2], in_=u_rows[0][:, 0:2, 0:2, :])
        load_g_scales(1)
        nc.sync.dma_start(out=u_first[0][:, 2:4], in_=u_rows[0][:, 2:4, 0:2, :])
        load_g(g_codes[1][:], 2, 4)
        nc.sync.dma_start(out=u_first[1][:], in_=u_rows[0][:, :, 2:4, :])
        nc.sync.dma_start(out=a_raw1[:], in_=a_rows[1])
        nc.sync.dma_start(out=u_second[:], in_=u_rows[1])

        mu_bank = next_bank()
        mu_words = mu_sb[:].bitcast(F32)
        for e in range(2):
            nc.tensor.transpose(mu_bank[:, e * P:(e + 1) * P], mu_words[:, e:e + 1].to_broadcast([P, P]), ident[:])
        for b in range(NB):
            nc.vector.tensor_scalar(out=row_rate[:, b, :, :], in0=lam_sb[:, :, 0:PACK], scalar1=kappa_sb[:, b:b + 1],
                                    scalar2=None, op0=ALU.add)
        nc.scalar.activation(out=ln_row[:].rearrange("p b g t -> p (b g t)"),
                             in_=row_rate[:].rearrange("p b g t -> p (b g t)"), func=ACT.Ln)
        nc.scalar.activation(out=ln_mu[:].rearrange("p (n e h) -> p n e h", e=2, h=2),
                             in_=mu_bank[:, 0:2 * P].bitcast(BF16).rearrange("p (e n h) -> p n e h", e=2, h=2), func=ACT.Ln)

        shares(0, 0, 8)
        shares(1, 0, 8)
        for t in range(PACK):
            turn_a(0, t)
        group_a(0, 0, nc.vector.tensor_copy)
        nc.vector.reciprocal(out=inv_row[:].rearrange("p b g t -> p (b g t)"),
                             in_=row_rate[:].rearrange("p b g t -> p (b g t)"))
        group_a(0, 1, nc.vector.tensor_copy)
        quantize_a(0, 0, 0, 2)
        group_a(0, 2, nc.vector.tensor_copy)
        group_a(0, 3, nc.vector.tensor_copy)
        quantize_a(0, 1, 0, 2)
        products(0, 0, 8)

        def divide_pair(c, n0, n1):
            for n in range(n0, n1):
                t, s = parts(c)[n]
                divide(c, t, s)
                if n < 3:
                    add_u(nc.gpsimd, c, t, t + 1, s, s + 1)

        def finish_pair(c, t0, t1, s0):
            add_u(nc.vector, c, max(t0, 1), t1, s0, 2)
            store_y(c, t0, t1, 0, 2)

        last = PAIRS - 1
        divide_pair(0, 0, 8)
        products(1, 0, 8)
        shares(2, 0, 5)
        finish_pair(0, 0, 2, 1)
        finish_pair(0, 2, 4, 0)
        group_y(0, 0, 0, NY, nc.scalar.copy)

        divide_pair(1, 0, 4)
        for slot in range(PACK):
            turn_a(1, slot)
            group_a(1, slot, nc.scalar.copy)
        group_y(0, 1, 0, NY, nc.scalar.copy)
        shares(2, 5, 8)
        divide_pair(1, 4, 8)
        quantize_a(1, 0, 0, 2)
        products(2, 0, 4)
        finish_pair(1, 0, 2, 1)
        quantize_y(0, 0)
        finish_pair(1, 2, 4, 0)
        quantize_a(1, 1, 0, 2)
        products(2, 4, 8)
        quantize_y(0, 1)
        store_codes(0, 0, 2)
        group_y(1, 0, 0, NY, nc.scalar.copy)
        group_y(1, 1, 0, NY, nc.scalar.copy)
        shares(3, 0, 8)

        divide_pair(2, 0, 8)
        products(3, 0, 8)
        quantize_y(1, 0)
        finish_pair(2, 0, 2, 1)
        quantize_y(1, 1)
        store_codes(1, 0, 2)
        store_scales(0, [nc.sync] * 4)
        finish_pair(2, 2, 4, 0)
        group_y(2, 0, 0, NY, nc.scalar.copy)
        group_y(2, 1, 0, NY, nc.scalar.copy)

        for n, (t, s) in enumerate(parts(last)):
            divide(last, t, s)
            if n == 0:
                add_u(nc.gpsimd, last, 0, 1, 0, 1)
                store_y(last, 0, 1, 0, 1)
            if n == 2:
                add_u(nc.gpsimd, last, 1, 3, 0, 1)
                store_y(last, 1, 3, 0, 1)
        add_u(nc.vector, last, 3, 4, 0, 1)
        store_y(last, 3, 4, 0, 1)
        group_y(last, 0, 0, NY, nc.scalar.copy)
        add_u(nc.vector, last, 0, 2, 1, 2)
        store_y(last, 0, 2, 1, 2)
        add_u(nc.vector, last, 2, 4, 1, 2)
        store_y(last, 2, 4, 1, 2)
        group_y(last, 1, CUT, NY, nc.scalar.copy)
        quantize_y(last - 1, 0)
        group_y(last, 1, 0, CUT, nc.vector.tensor_copy)
        quantize_y(last - 1, 1)
        store_codes(last - 1, 0, 2)
        quantize_y(last, 0)
        store_codes(last, 0, 1)
        quantize_y(last, 1)
        store_codes(last, 1, 2)
        store_scales(1, [nc.sync, nc.sync, nc.scalar, nc.scalar])
